import numpy as np
import ml_dtypes


def mxq(x, axis, fmt="e4m3"):
    dtype, down = {"e4m3": (ml_dtypes.float8_e4m3fn, 7), "e5m2": (ml_dtypes.float8_e5m2, 14)}[fmt]
    v = np.moveaxis(np.asarray(x, np.float32).astype(ml_dtypes.bfloat16).astype(np.float64), axis, -1)
    blocks = v.reshape(v.shape[:-1] + (-1, 32))
    amax = np.abs(blocks).max(-1, keepdims=True)
    byte = np.maximum(np.where(amax > 0, np.frexp(amax)[1] - 1 + 127, 0) - down, 1)
    scale = np.exp2(byte - 127.0)
    codes = (blocks / scale).astype(np.float32).astype(dtype).astype(np.float64)
    return np.moveaxis((codes * scale).reshape(v.shape), -1, axis)


WIDE = False


def mx_kscale(k):
    if not WIDE:
        return np.ones(k)
    levels = np.array([10, -10, 5, -5, 0])
    if k % 512:
        return np.exp2(np.random.permutation(np.resize(levels, k // 32))).repeat(32)
    a = np.empty((k // 512, 16))
    for p in range(k // 512):
        a[p, :8] = np.random.permutation(np.resize(levels, 8))
        for g in range(8):
            far = levels[np.abs(levels - a[p, g]) >= 10]
            a[p, g + 8] = far[np.random.randint(len(far))]
    return np.exp2(a.ravel()).repeat(32)


def f64(x):
    return np.asarray(x).astype(np.float64)


def striped(idx):
    return np.tile(idx.reshape(-1, 16).T, (8, 1)).astype(np.uint16)


def unstriped(offs):
    return offs[:16].T.reshape(-1).astype(np.int64)


def pack_weight(w):
    k, n = w.shape
    w = f64(np.asarray(w, np.float32).astype(ml_dtypes.bfloat16)).reshape(k // 32, 32, n)
    amax = np.abs(w).max(1)
    byte = np.clip(np.where(amax > 0, np.frexp(amax)[1] - 1 + 127 - 7, 1), 1, 254)
    scaled = (w * np.exp2(127.0 - byte)[:, None, :]).reshape(k, n).astype(np.float32)
    words = np.ascontiguousarray(scaled.reshape(k // 512, 128, 4, n).transpose(0, 1, 3, 2)).astype(ml_dtypes.float8_e4m3fn).view(np.uint8)
    return words, np.ascontiguousarray(byte.astype(np.uint8).reshape(k // 512, 16, n))


def unpack_weight(words, scales):
    g, p, n, _ = words.shape
    vals = np.ascontiguousarray(words).view(ml_dtypes.float8_e4m3fn).astype(np.float64) * np.repeat(np.exp2(scales.astype(np.float64) - 127.0), 8, axis=1)[..., None]
    return vals.transpose(0, 1, 3, 2).reshape(g * 512, n)


def relu(v):
    return np.maximum(v, 0.0)


def sigmoid(v):
    return 1.0 / (1.0 + np.exp(-np.maximum(v, -700.0)))


K, T, S, D, N, H, V, W, U = 512, 4096, 1024, 4, 128, 512, 256, 1024, 512


def setup_inputs():
    n = np.random.standard_normal
    s = mx_kscale(K)[:, None]
    u = mx_kscale(H)
    packed_xT = pack_weight(n((K, T)) * s)
    packed_eT = pack_weight(n((K, W)) * s)
    return {
        "x_words": packed_xT[0],
        "x_scales": packed_xT[1],
        "w1": (n((K, H)) / np.sqrt(K) / s).astype(np.float32),
        "e_words": packed_eT[0],
        "e_scales": packed_eT[1],
        "w2": (n((K, H)) / np.sqrt(K) / s).astype(np.float32),
        "wp": (n((H, 1))).astype(np.float32),
        "wd": (n((H, 1))).astype(np.float32),
        "unit": (np.random.uniform(0.6, 1.4, (H, 1)) * u[:, None]).astype(np.float32),
        "w3": (n((H, N)) / np.sqrt(H) / u[:, None]).astype(np.float32),
        "offs": striped(np.random.permutation(T)[:S]),
        "tgt": striped(np.random.permutation(W)[:V]),
        "imp": striped(np.random.permutation(np.concatenate([np.arange(V), np.random.randint(0, V, U - V)]))),
    }


def reference(x_words, x_scales, w1, e_words, e_scales, w2, wp, wd, unit, w3, offs, tgt, imp):
    xq = unpack_weight(x_words, x_scales)[:, unstriped(offs)]
    y = mxq(f64(w1), 0, "e4m3").T @ xq
    e_tgt = unpack_weight(e_words, e_scales)[:, unstriped(tgt)]
    ye = mxq(f64(w2), 0, "e4m3").T @ e_tgt
    att = sigmoid(f64(wp) * (y * np.repeat(ye, D, axis=1)) + f64(wd) * (y - np.repeat(ye, D, axis=1)))
    ay = att * y
    user = ay.reshape(len(ay), -1, D).sum(axis=2)
    ui = user[:, unstriped(imp)]
    hid = f64(unit) * (relu(ui - ye[:, unstriped(imp)]))
    return mxq(f64(w3), 0, "e4m3").T @ mxq(hid, 0, "e4m3")

@@ -1,0 +1,250 @@
+from contextlib import ExitStack
+
+import concourse.mybir as mybir
+from concourse.masks import make_identity
+
+F32 = mybir.dt.float32
+BF16 = mybir.dt.bfloat16
+I32 = mybir.dt.int32
+U32 = mybir.dt.uint32
+U16 = mybir.dt.uint16
+U8 = mybir.dt.uint8
+FP8X4 = mybir.dt.float8_e4m3fn_x4
+ALU = mybir.AluOpType
+ACT = mybir.ActivationFunctionType
+
+P = 128
+PACK = 4
+K, T, S, D, N, H, V, W, U = 512, 4096, 1024, 4, 128, 512, 256, 1024, 512
+HALF = 128
+WINDOW = 704
+ON_VECTOR = (0,)
+FLOPS = 2 * K * H * S + 2 * K * H * V + 2 * H * N * U
+
+
+def tile_picked_ydintg_dif_p_kernel(
+    tc, x_words, x_scales, w1, e_words, e_scales, w2, wp, wd, unit, w3, offs, tgt, imp, out
+):
+    nc = tc.nc
+    with ExitStack() as ctx:
+        keep = ctx.enter_context(tc.tile_pool(name="keep", bufs=1))
+        ring = ctx.enter_context(tc.tile_pool(name="ring", bufs=6))
+        psum = ctx.enter_context(tc.psum_pool(name="psum", bufs=1))
+
+        offs_sb = keep.tile([P, S // 16], U16, name="offs_sb")
+        tgt_sb = keep.tile([P, V // 16], U16, name="tgt_sb")
+        imp_sb = keep.tile([P, U // 16], U16, name="imp_sb")
+        nc.sync.dma_start(offs_sb[:], offs)
+        nc.sync.dma_start(tgt_sb[:], tgt)
+        nc.sync.dma_start(imp_sb[:], imp)
+
+        e_table = keep.tile([P, W], I32, name="e_table")
+        nc.sync.dma_start(e_table[:], e_words[0].rearrange("p n t -> p (n t)").bitcast(I32))
+        w2_raw = keep.tile([P, PACK, H], F32, name="w2_raw")
+        nc.sync.dma_start(w2_raw[:], w2.rearrange("(p j) c -> p j c", j=PACK))
+        e_scale_table = keep.tile([P, W], U8, name="e_scale_table")
+        nc.vector.memset(e_scale_table[:].bitcast(I32), 0)
+        x_scale_table = keep.tile([P, T], U8, name="x_scale_table")
+        nc.vector.memset(x_scale_table[:].bitcast(I32), 0)
+        nc.scalar.dma_start(e_scale_table[0:P:8, :].bitcast(I32), e_scales[0].bitcast(I32))
+        nc.scalar.dma_start(x_scale_table[0:P:8, :].bitcast(I32), x_scales[0].bitcast(I32))
+        warm_in = keep.tile([P, 1], F32, name="warm_in", tag="x_table")
+        warm_out = keep.tile([P, 1], F32, name="warm_out", tag="w1_raw")
+        nc.vector.memset(warm_in[:], 0.0)
+        nc.scalar.activation(warm_out[:], warm_in[:], ACT.Sigmoid)
+        x_table = keep.tile([P, T], I32, name="x_table", tag="x_table")
+        nc.sync.dma_start(x_table[:], x_words[0].rearrange("p n t -> p (n t)").bitcast(I32))
+        w1_raw = keep.tile([P, PACK, H], F32, name="w1_raw", tag="w1_raw")
+        nc.sync.dma_start(w1_raw[:], w1.rearrange("(p j) c -> p j c", j=PACK))
+        scale_plane = keep.tile([P, S + V], U8, name="scale_plane", align_bytes=64)
+        nc.vector.memset(scale_plane[:].bitcast(I32), 0)
+        x_scale_plane = scale_plane[:, 0:S]
+        e_scale_plane = scale_plane[:, S : S + V]
+
+        wp_sb = keep.tile([P, PACK], F32, name="wp_sb")
+        wd_sb = keep.tile([P, PACK], F32, name="wd_sb")
+        unit_sb = keep.tile([P, PACK], F32, name="unit_sb")
+        nc.gpsimd.dma_start(wp_sb[:], wp.rearrange("(p t) o -> p (t o)", t=PACK))
+        nc.gpsimd.dma_start(wd_sb[:], wd.rearrange("(p t) o -> p (t o)", t=PACK))
+        nc.gpsimd.dma_start(unit_sb[:], unit.rearrange("(p t) o -> p (t o)", t=PACK))
+        ident = keep.tile([P, P], F32, name="ident")
+        make_identity(nc, ident[:])
+        hid_v = keep.tile([P, (PACK - 1) * V + WINDOW], F32, name="hid_v")
+        nc.gpsimd.memset(hid_v[:, PACK * V :], 0.0)
+
+        e_codes = keep.tile([P, V], U32, name="e_codes", align_bytes=64)
+        nc.vector.tensor_copy(e_codes[:], e_table[:].bitcast(U32).indirect(tgt_sb[:]))
+        scale_picked = keep.tile([P, S + V], U8, name="scale_picked")
+        nc.vector.tensor_copy(scale_picked[:, S : S + V], e_scale_table[:].indirect(tgt_sb[:]))
+        nc.vector.tensor_copy(scale_picked[:, 0:S], x_scale_table[:].indirect(offs_sb[:]))
+        for q in range(4):
+            nc.scalar.dma_start(
+                scale_plane[32 * q : 32 * q + 4, :].bitcast(I32),
+                scale_picked[32 * q : 32 * q + 32 : 8, :].bitcast(I32),
+            )
+
+        w2_bf = keep.tile([P, PACK, P, PACK], BF16, name="w2_bf", tag="w_second", align_bytes=64)
+        nc.vector.tensor_copy(
+            w2_bf[:].rearrange("p t m j -> p m j t"), w2_raw[:].rearrange("p j (m t) -> p m j t", t=PACK)
+        )
+        w2_codes = keep.tile([P, H], U32, name="w2_codes", align_bytes=64)
+        w2_scales = keep.tile([P, H], U8, name="w2_scales", align_bytes=64)
+        nc.vector.quantize_mx(w2_codes[:].bitcast(FP8X4), w2_scales[:], w2_bf[:].rearrange("p t m j -> p (t m j)"))
+
+        w3_raw = keep.tile([P, PACK, N], F32, name="w3_raw", tag="w_second", align_bytes=64)
+        nc.sync.dma_start(w3_raw[:], w3.rearrange("(p j) c -> p j c", j=PACK))
+
+        neg_ye = keep.tile([P, PACK, V], F32, name="neg_ye")
+        slope = keep.tile([P, PACK, V], F32, name="slope")
+        shift = keep.tile([P, PACK, V], F32, name="shift")
+        ye_banks = []
+        for pair in range(2):
+            ye = psum.tile([P, 2, V], F32, name="ye", tag="turned", bufs=3)
+            ye_banks.append(ye)
+            for s in range(2):
+                cols = slice((2 * pair + s) * P, (2 * pair + s + 1) * P)
+                nc.tensor.matmul_mx(
+                    ye[:, s, :], lhsT=w2_codes[:, cols].bitcast(FP8X4), lhsT_scale=w2_scales[:, cols],
+                    rhs=e_codes[:].bitcast(FP8X4), rhs_scale=e_scale_plane, start=True, stop=True,
+                )
+            nc.scalar.activation(neg_ye[:, 2 * pair : 2 * pair + 2, :], ye[:], ACT.Copy, scale=-1.0)
+            for s in range(2):
+                t = 2 * pair + s
+                nc.scalar.activation(
+                    slope[:, t, :], ye[:, s, :], ACT.Identity, bias=wd_sb[:, t : t + 1], scale=wp_sb[:, t : t + 1]
+                )
+                nc.gpsimd.tensor_scalar(shift[:, t, :], neg_ye[:, t, :], wd_sb[:, t : t + 1], 0.0, ALU.mult, ALU.add)
+
+        x_codes = keep.tile([P, S], U32, name="x_codes", align_bytes=64)
+        nc.vector.tensor_copy(x_codes[:], x_table[:].bitcast(U32).indirect(offs_sb[:]))
+
+        w1_bf = keep.tile([P, PACK, P, PACK], BF16, name="w1_bf", align_bytes=64)
+        w1_view = w1_raw[:].rearrange("p j (m t) -> p m j t", t=PACK)
+        nc.vector.tensor_copy(w1_bf[:, 0, :, :], w1_view[:, :, :, 0])
+        nc.scalar.copy(w1_bf[:, 1:PACK, :, :].rearrange("p t m j -> p m j t"), w1_view[:, :, :, 1:PACK])
+        w1_codes = keep.tile([P, H], U32, name="w1_codes", align_bytes=64)
+        w1_scales = keep.tile([P, H], U8, name="w1_scales", align_bytes=64)
+
+        def quantize_w1(t):
+            cols = slice(t * P, (t + 1) * P)
+            nc.vector.quantize_mx(
+                w1_codes[:, cols].bitcast(FP8X4), w1_scales[:, cols], w1_bf[:, t, :, :].rearrange("p m j -> p (m j)")
+            )
+
+        quantize_w1(0)
+
+        w3_bf = keep.tile([P, N, PACK], BF16, name="w3_bf", align_bytes=64)
+        w3_codes = keep.tile([P, N], U32, name="w3_codes", align_bytes=64)
+        w3_scales = keep.tile([P, N], U8, name="w3_scales", align_bytes=64)
+
+        picked = keep.tile([P, PACK, U], F32, name="picked")
+        ys = {}
+        atts = {}
+
+        def over_d(ap):
+            return ap.unsqueeze(1).to_broadcast([P, D, HALF])
+
+        def front(u):
+            t, h = divmod(u, 2)
+            cols = slice(t * P, (t + 1) * P)
+            js = slice(h * HALF * D, (h + 1) * HALF * D)
+            vs = slice(h * HALF, (h + 1) * HALF)
+            y = psum.tile([P, HALF * D], F32, name="y", tag="y", bufs=5)
+            nc.tensor.matmul_mx(
+                y[:], lhsT=w1_codes[:, cols].bitcast(FP8X4), lhsT_scale=w1_scales[:, cols],
+                rhs=x_codes[:, js].bitcast(FP8X4), rhs_scale=x_scale_plane[:, js], start=True, stop=True,
+            )
+            ys[u] = y[:].rearrange("p (v d) -> p d v", d=D)
+            prod = ring.tile([P, D, HALF], F32, name="prod")
+            nc.vector.tensor_tensor(prod[:], ys[u], over_d(slope[:, t, vs]), ALU.mult)
+            logit = ring.tile([P, D, HALF], F32, name="logit")
+            if u == units - 1:
+                att = picked[:, 1, :].rearrange("p (d v) -> p d v", d=D)
+            else:
+                att = ring.tile([P, D, HALF], F32, name="att")
+            if u in ON_VECTOR:
+                nc.vector.scalar_tensor_tensor(
+                    logit[:], over_d(ye_banks[0][:, t, vs]), wd_sb[:, t : t + 1], prod[:], ALU.mult, ALU.subtract
+                )
+                nc.scalar.activation(att[:], logit[:], ACT.Sigmoid, scale=-1.0)
+            else:
+                nc.gpsimd.tensor_tensor(logit[:], prod[:], over_d(shift[:, t, vs]), ALU.add)
+                nc.scalar.activation(att[:], logit[:], ACT.Sigmoid)
+            atts[u] = att
+
+        ays = {}
+        positives = {}
+
+        def weigh(u):
+            ay = ring.tile([P, D, HALF], F32, name="ay")
+            nc.vector.tensor_tensor(ay[:], ys[u], atts[u][:], ALU.mult)
+            ays[u] = ay
+
+        def turn(u):
+            bank = psum.tile([P, 2, P], F32, name="bank", tag="turned", bufs=3)
+            if u < units:
+                t, h = divmod(u, 2)
+                vs = slice(h * HALF, (h + 1) * HALF)
+                nc.tensor.matmul(bank[:, 0, :], neg_ye[:, t, vs], ident[:], start=True, stop=False, is_transpose=True)
+                for d in range(D):
+                    nc.tensor.matmul(
+                        bank[:, 0, :], ays[u][:, d, :], ident[:], start=False, stop=(d == D - 1), is_transpose=True
+                    )
+            if u > 0:
+                nc.tensor.transpose(bank[:, 1, :], positives[u - 1][:], ident[:])
+            if u < units:
+                pos = ring.tile([P, P], F32, name="pos")
+                nc.scalar.activation(pos[:], bank[:, 0, :], ACT.Relu)
+                positives[u] = pos
+            if u > 0:
+                t, h = divmod(u - 1, 2)
+                c0 = (PACK - 1 - t) * V + h * HALF
+                nc.scalar.activation(hid_v[:, c0 : c0 + HALF], bank[:, 1, :], ACT.Copy, scale=unit_sb[:, t : t + 1])
+
+        units = 2 * PACK
+        weigh_lag = 2
+        turn_lag = 5
+        for step in range(units + turn_lag + 1):
+            if step < units:
+                front(step)
+            if step == 0:
+                for t in range(1, PACK):
+                    quantize_w1(t)
+            if weigh_lag <= step < units + weigh_lag:
+                weigh(step - weigh_lag)
+            if step >= turn_lag:
+                turn(step - turn_lag)
+            if step == units - 1:
+                nc.scalar.copy(w3_bf[:], w3_raw[:].rearrange("p j n -> p n j"))
+                nc.vector.quantize_mx(w3_codes[:].bitcast(FP8X4), w3_scales[:], w3_bf[:].rearrange("p n j -> p (n j)"))
+
+        hid_bf = keep.tile([P, U, PACK], BF16, name="hid_bf", align_bytes=64)
+        halves = [slice(h * U // 2, (h + 1) * U // 2) for h in range(2)]
+        for t in range(PACK - 1):
+            c0 = (PACK - 1 - t) * V
+            nc.vector.tensor_copy(picked[:, t, :], hid_v[:, c0 : c0 + WINDOW].indirect(imp_sb[:]))
+        for h, rs in enumerate(halves):
+            nc.vector.tensor_copy(picked[:, PACK - 1, rs], hid_v[:, 0:U].indirect(imp_sb[:, h * 16 : (h + 1) * 16]))
+        nc.scalar.copy(hid_bf[:, halves[0], :], picked[:, :, halves[0]].rearrange("p t r -> p r t"))
+        nc.vector.tensor_copy(hid_bf[:, halves[1], :], picked[:, :, halves[1]].rearrange("p t r -> p r t"))
+
+        hid_codes = keep.tile([P, U], U32, name="hid_codes", align_bytes=64)
+        hid_scales = keep.tile([P, U], U8, name="hid_scales", align_bytes=64)
+        for h in range(2):
+            rs = slice(h * U // 2, (h + 1) * U // 2)
+            nc.vector.quantize_mx(
+                hid_codes[:, rs].bitcast(FP8X4), hid_scales[:, rs], hid_bf[:, rs, :].rearrange("p r t -> p (r t)")
+            )
+        for h in range(2):
+            rs = slice(h * U // 2, (h + 1) * U // 2)
+            acc = psum.tile([P, U // 2], F32, name="acc", tag="y", bufs=5)
+            nc.tensor.matmul_mx(
+                acc[:], lhsT=w3_codes[:].bitcast(FP8X4), lhsT_scale=w3_scales[:],
+                rhs=hid_codes[:, rs].bitcast(FP8X4), rhs_scale=hid_scales[:, rs], start=True, stop=True,
+            )
+            res = keep.tile([P, U // 2], F32, name="res%d" % h)
+            if h == 0:
+                nc.scalar.copy(res[:], acc[:])
+            else:
+                nc.vector.tensor_copy(res[:], acc[:])
+            nc.sync.dma_start(out[:, rs], res[:])

@@ -17,8 +17,8 @@ P = 128
 PACK = 4
 K, T, S, D, N, H, V, W, U = 512, 4096, 1024, 4, 128, 512, 256, 1024, 512
 HALF = 128
-WINDOW = 704
-ON_VECTOR = (0,)
+WINDOW = 512
+ON_VECTOR = (0, 3)
 FLOPS = 2 * K * H * S + 2 * K * H * V + 2 * H * N * U
 
 
@@ -34,32 +34,35 @@ def tile_picked_ydintg_dif_p_kernel(
         offs_sb = keep.tile([P, S // 16], U16, name="offs_sb")
         tgt_sb = keep.tile([P, V // 16], U16, name="tgt_sb")
         imp_sb = keep.tile([P, U // 16], U16, name="imp_sb")
-        nc.sync.dma_start(offs_sb[:], offs)
         nc.sync.dma_start(tgt_sb[:], tgt)
-        nc.sync.dma_start(imp_sb[:], imp)
+        nc.sync.dma_start(offs_sb[:], offs)
 
+        x_scale_table = keep.tile([P, T], U8, name="x_scale_table")
+        nc.vector.memset(x_scale_table[:, 0 : T // 2].bitcast(I32), 0)
+        nc.gpsimd.memset(x_scale_table[:, T // 2 : T].bitcast(I32), 0)
+        nc.sync.dma_start(x_scale_table[0:P:8, :].bitcast(I32), x_scales[0].bitcast(I32))
         e_table = keep.tile([P, W], I32, name="e_table")
         nc.sync.dma_start(e_table[:], e_words[0].rearrange("p n t -> p (n t)").bitcast(I32))
         w2_raw = keep.tile([P, PACK, H], F32, name="w2_raw")
         nc.sync.dma_start(w2_raw[:], w2.rearrange("(p j) c -> p j c", j=PACK))
         e_scale_table = keep.tile([P, W], U8, name="e_scale_table")
-        nc.vector.memset(e_scale_table[:].bitcast(I32), 0)
-        x_scale_table = keep.tile([P, T], U8, name="x_scale_table")
-        nc.vector.memset(x_scale_table[:].bitcast(I32), 0)
-        nc.scalar.dma_start(e_scale_table[0:P:8, :].bitcast(I32), e_scales[0].bitcast(I32))
-        nc.scalar.dma_start(x_scale_table[0:P:8, :].bitcast(I32), x_scales[0].bitcast(I32))
-        warm_in = keep.tile([P, 1], F32, name="warm_in", tag="x_table")
-        warm_out = keep.tile([P, 1], F32, name="warm_out", tag="w1_raw")
+        nc.gpsimd.memset(e_scale_table[:].bitcast(I32), 0)
+        for q in range(4):
+            nc.sync.dma_start(
+                e_scale_table[32 * q : 32 * q + 4, :].bitcast(I32), e_scales[0, 4 * q : 4 * q + 4, :].bitcast(I32)
+            )
+        nc.sync.dma_start(imp_sb[:], imp)
+
+        warm_in = keep.tile([P, 1], F32, name="warm_in", tag="w1_raw")
+        warm_out = keep.tile([P, 1], F32, name="warm_out", tag="x_table")
         nc.vector.memset(warm_in[:], 0.0)
         nc.scalar.activation(warm_out[:], warm_in[:], ACT.Sigmoid)
-        x_table = keep.tile([P, T], I32, name="x_table", tag="x_table")
-        nc.sync.dma_start(x_table[:], x_words[0].rearrange("p n t -> p (n t)").bitcast(I32))
         w1_raw = keep.tile([P, PACK, H], F32, name="w1_raw", tag="w1_raw")
         nc.sync.dma_start(w1_raw[:], w1.rearrange("(p j) c -> p j c", j=PACK))
-        scale_plane = keep.tile([P, S + V], U8, name="scale_plane", align_bytes=64)
-        nc.vector.memset(scale_plane[:].bitcast(I32), 0)
-        x_scale_plane = scale_plane[:, 0:S]
-        e_scale_plane = scale_plane[:, S : S + V]
+        x_table = keep.tile([P, T], I32, name="x_table", tag="x_table")
+        nc.sync.dma_start(x_table[:], x_words[0].rearrange("p n t -> p (n t)").bitcast(I32))
+        x_scale_plane = keep.tile([P, S], U8, name="x_scale_plane", align_bytes=64)
+        nc.vector.memset(x_scale_plane[:].bitcast(I32), 0)
 
         wp_sb = keep.tile([P, PACK], F32, name="wp_sb")
         wd_sb = keep.tile([P, PACK], F32, name="wd_sb")
@@ -72,16 +75,17 @@ def tile_picked_ydintg_dif_p_kernel(
         hid_v = keep.tile([P, (PACK - 1) * V + WINDOW], F32, name="hid_v")
         nc.gpsimd.memset(hid_v[:, PACK * V :], 0.0)
 
+        x_scale_picked = keep.tile([P, S], U8, name="x_scale_picked")
+        nc.vector.tensor_copy(x_scale_picked[:], x_scale_table[:].indirect(offs_sb[:]))
+        for q in range(4):
+            nc.sync.dma_start(
+                x_scale_plane[32 * q : 32 * q + 4, :].bitcast(I32),
+                x_scale_picked[32 * q : 32 * q + 32 : 8, :].bitcast(I32),
+            )
         e_codes = keep.tile([P, V], U32, name="e_codes", align_bytes=64)
         nc.vector.tensor_copy(e_codes[:], e_table[:].bitcast(U32).indirect(tgt_sb[:]))
-        scale_picked = keep.tile([P, S + V], U8, name="scale_picked")
-        nc.vector.tensor_copy(scale_picked[:, S : S + V], e_scale_table[:].indirect(tgt_sb[:]))
-        nc.vector.tensor_copy(scale_picked[:, 0:S], x_scale_table[:].indirect(offs_sb[:]))
-        for q in range(4):
-            nc.scalar.dma_start(
-                scale_plane[32 * q : 32 * q + 4, :].bitcast(I32),
-                scale_picked[32 * q : 32 * q + 32 : 8, :].bitcast(I32),
-            )
+        e_scale_plane = keep.tile([P, V], U8, name="e_scale_plane", align_bytes=64)
+        nc.vector.tensor_copy(e_scale_plane[:], e_scale_table[:].indirect(tgt_sb[:]))
 
         w2_bf = keep.tile([P, PACK, P, PACK], BF16, name="w2_bf", tag="w_second", align_bytes=64)
         nc.vector.tensor_copy(
@@ -105,7 +109,7 @@ def tile_picked_ydintg_dif_p_kernel(
                 cols = slice((2 * pair + s) * P, (2 * pair + s + 1) * P)
                 nc.tensor.matmul_mx(
                     ye[:, s, :], lhsT=w2_codes[:, cols].bitcast(FP8X4), lhsT_scale=w2_scales[:, cols],
-                    rhs=e_codes[:].bitcast(FP8X4), rhs_scale=e_scale_plane, start=True, stop=True,
+                    rhs=e_codes[:].bitcast(FP8X4), rhs_scale=e_scale_plane[:], start=True, stop=True,
                 )
             nc.scalar.activation(neg_ye[:, 2 * pair : 2 * pair + 2, :], ye[:], ACT.Copy, scale=-1.0)
             for s in range(2):
@@ -113,27 +117,25 @@ def tile_picked_ydintg_dif_p_kernel(
                 nc.scalar.activation(
                     slope[:, t, :], ye[:, s, :], ACT.Identity, bias=wd_sb[:, t : t + 1], scale=wp_sb[:, t : t + 1]
                 )
-                nc.gpsimd.tensor_scalar(shift[:, t, :], neg_ye[:, t, :], wd_sb[:, t : t + 1], 0.0, ALU.mult, ALU.add)
-
-        x_codes = keep.tile([P, S], U32, name="x_codes", align_bytes=64)
-        nc.vector.tensor_copy(x_codes[:], x_table[:].bitcast(U32).indirect(offs_sb[:]))
+                for h in range(2):
+                    if 2 * t + h not in ON_VECTOR:
+                        vs = slice(h * HALF, (h + 1) * HALF)
+                        nc.scalar.activation(shift[:, t, vs], ye[:, s, vs], ACT.Copy, scale=wd_sb[:, t : t + 1])
 
         w1_bf = keep.tile([P, PACK, P, PACK], BF16, name="w1_bf", align_bytes=64)
-        w1_view = w1_raw[:].rearrange("p j (m t) -> p m j t", t=PACK)
-        nc.vector.tensor_copy(w1_bf[:, 0, :, :], w1_view[:, :, :, 0])
-        nc.scalar.copy(w1_bf[:, 1:PACK, :, :].rearrange("p t m j -> p m j t"), w1_view[:, :, :, 1:PACK])
+        nc.vector.tensor_copy(
+            w1_bf[:].rearrange("p t m j -> p m j t"), w1_raw[:].rearrange("p j (m t) -> p m j t", t=PACK)
+        )
         w1_codes = keep.tile([P, H], U32, name="w1_codes", align_bytes=64)
         w1_scales = keep.tile([P, H], U8, name="w1_scales", align_bytes=64)
+        nc.vector.quantize_mx(w1_codes[:].bitcast(FP8X4), w1_scales[:], w1_bf[:].rearrange("p t m j -> p (t m j)"))
 
-        def quantize_w1(t):
-            cols = slice(t * P, (t + 1) * P)
-            nc.vector.quantize_mx(
-                w1_codes[:, cols].bitcast(FP8X4), w1_scales[:, cols], w1_bf[:, t, :, :].rearrange("p m j -> p (m j)")
+        x_codes = keep.tile([P, S], U32, name="x_codes", align_bytes=64)
+        for h in range(2):
+            nc.vector.tensor_copy(
+                x_codes[:, h * 512 : (h + 1) * 512], x_table[:].bitcast(U32).indirect(offs_sb[:, h * 32 : (h + 1) * 32])
             )
 
-        quantize_w1(0)
-
-        w3_bf = keep.tile([P, N, PACK], BF16, name="w3_bf", align_bytes=64)
         w3_codes = keep.tile([P, N], U32, name="w3_codes", align_bytes=64)
         w3_scales = keep.tile([P, N], U8, name="w3_scales", align_bytes=64)
 
@@ -155,12 +157,16 @@ def tile_picked_ydintg_dif_p_kernel(
                 rhs=x_codes[:, js].bitcast(FP8X4), rhs_scale=x_scale_plane[:, js], start=True, stop=True,
             )
             ys[u] = y[:].rearrange("p (v d) -> p d v", d=D)
-            prod = ring.tile([P, D, HALF], F32, name="prod")
-            nc.vector.tensor_tensor(prod[:], ys[u], over_d(slope[:, t, vs]), ALU.mult)
-            logit = ring.tile([P, D, HALF], F32, name="logit")
             if u == units - 1:
-                att = picked[:, 1, :].rearrange("p (d v) -> p d v", d=D)
+                prod = keep.tile([P, D, HALF], F32, name="last_prod", tag="last_prod", align_bytes=64)
             else:
+                prod = ring.tile([P, D, HALF], F32, name="prod")
+            nc.vector.tensor_tensor(prod[:], ys[u], over_d(slope[:, t, vs]), ALU.mult)
+            if u == units - 1:
+                logit = picked[:, 1, :].rearrange("p (d v) -> p d v", d=D)
+                att = picked[:, 0, :].rearrange("p (d v) -> p d v", d=D)
+            else:
+                logit = ring.tile([P, D, HALF], F32, name="logit")
                 att = ring.tile([P, D, HALF], F32, name="att")
             if u in ON_VECTOR:
                 nc.vector.scalar_tensor_tensor(
@@ -168,7 +174,7 @@ def tile_picked_ydintg_dif_p_kernel(
                 )
                 nc.scalar.activation(att[:], logit[:], ACT.Sigmoid, scale=-1.0)
             else:
-                nc.gpsimd.tensor_tensor(logit[:], prod[:], over_d(shift[:, t, vs]), ALU.add)
+                nc.gpsimd.tensor_tensor(logit[:], prod[:], over_d(shift[:, t, vs]), ALU.subtract)
                 nc.scalar.activation(att[:], logit[:], ACT.Sigmoid)
             atts[u] = att
 
@@ -207,26 +213,26 @@ def tile_picked_ydintg_dif_p_kernel(
         for step in range(units + turn_lag + 1):
             if step < units:
                 front(step)
-            if step == 0:
-                for t in range(1, PACK):
-                    quantize_w1(t)
             if weigh_lag <= step < units + weigh_lag:
                 weigh(step - weigh_lag)
             if step >= turn_lag:
                 turn(step - turn_lag)
             if step == units - 1:
+                w3_bf = keep.tile([P, N, PACK], BF16, name="w3_bf", tag="last_prod", align_bytes=64)
                 nc.scalar.copy(w3_bf[:], w3_raw[:].rearrange("p j n -> p n j"))
                 nc.vector.quantize_mx(w3_codes[:].bitcast(FP8X4), w3_scales[:], w3_bf[:].rearrange("p n j -> p (n j)"))
 
         hid_bf = keep.tile([P, U, PACK], BF16, name="hid_bf", align_bytes=64)
         halves = [slice(h * U // 2, (h + 1) * U // 2) for h in range(2)]
-        for t in range(PACK - 1):
+        for t, h in ((0, 0), (1, 0), (2, 0), (0, 1), (3, 0), (1, 1), (2, 1), (3, 1)):
             c0 = (PACK - 1 - t) * V
-            nc.vector.tensor_copy(picked[:, t, :], hid_v[:, c0 : c0 + WINDOW].indirect(imp_sb[:]))
-        for h, rs in enumerate(halves):
-            nc.vector.tensor_copy(picked[:, PACK - 1, rs], hid_v[:, 0:U].indirect(imp_sb[:, h * 16 : (h + 1) * 16]))
-        nc.scalar.copy(hid_bf[:, halves[0], :], picked[:, :, halves[0]].rearrange("p t r -> p r t"))
-        nc.vector.tensor_copy(hid_bf[:, halves[1], :], picked[:, :, halves[1]].rearrange("p t r -> p r t"))
+            nc.vector.tensor_copy(
+                picked[:, t, halves[h]], hid_v[:, c0 : c0 + WINDOW].indirect(imp_sb[:, h * 16 : (h + 1) * 16])
+            )
+        planes = picked[:].rearrange("p t r -> p r t")
+        nc.scalar.copy(hid_bf[:, 0:256, :], planes[:, 0:256, :])
+        nc.scalar.copy(hid_bf[:, 256:352, :], planes[:, 256:352, :])
+        nc.vector.tensor_copy(hid_bf[:, 352:512, :], planes[:, 352:512, :])
 
         hid_codes = keep.tile([P, U], U32, name="hid_codes", align_bytes=64)
         hid_scales = keep.tile([P, U], U8, name="hid_scales", align_bytes=64)

@@ -18,7 +18,7 @@ PACK = 4
 K, T, S, D, N, H, V, W, U = 512, 4096, 1024, 4, 128, 512, 256, 1024, 512
 HALF = 128
 WINDOW = 512
-ON_VECTOR = (0, 3)
+ON_VECTOR = (1, 3)
 FLOPS = 2 * K * H * S + 2 * K * H * V + 2 * H * N * U
 
 
@@ -38,17 +38,17 @@ def tile_picked_ydintg_dif_p_kernel(
         nc.sync.dma_start(offs_sb[:], offs)
 
         x_scale_table = keep.tile([P, T], U8, name="x_scale_table")
-        nc.vector.memset(x_scale_table[:, 0 : T // 2].bitcast(I32), 0)
-        nc.gpsimd.memset(x_scale_table[:, T // 2 : T].bitcast(I32), 0)
-        nc.sync.dma_start(x_scale_table[0:P:8, :].bitcast(I32), x_scales[0].bitcast(I32))
+        nc.vector.memset(x_scale_table[:].bitcast(I32), 0)
+        e_scale_table = keep.tile([P, W], U8, name="e_scale_table")
+        nc.gpsimd.memset(e_scale_table[:].bitcast(I32), 0)
         e_table = keep.tile([P, W], I32, name="e_table")
         nc.sync.dma_start(e_table[:], e_words[0].rearrange("p n t -> p (n t)").bitcast(I32))
         w2_raw = keep.tile([P, PACK, H], F32, name="w2_raw")
         nc.sync.dma_start(w2_raw[:], w2.rearrange("(p j) c -> p j c", j=PACK))
-        e_scale_table = keep.tile([P, W], U8, name="e_scale_table")
-        nc.gpsimd.memset(e_scale_table[:].bitcast(I32), 0)
+        nc.sync.dma_start(x_scale_table[0:P:8, :].bitcast(I32), x_scales[0].bitcast(I32))
         for q in range(4):
-            nc.sync.dma_start(
+            queue = nc.gpsimd if q == 3 else nc.sync
+            queue.dma_start(
                 e_scale_table[32 * q : 32 * q + 4, :].bitcast(I32), e_scales[0, 4 * q : 4 * q + 4, :].bitcast(I32)
             )
         nc.sync.dma_start(imp_sb[:], imp)
@@ -88,7 +88,7 @@ def tile_picked_ydintg_dif_p_kernel(
         nc.vector.tensor_copy(e_scale_plane[:], e_scale_table[:].indirect(tgt_sb[:]))
 
         w2_bf = keep.tile([P, PACK, P, PACK], BF16, name="w2_bf", tag="w_second", align_bytes=64)
-        nc.vector.tensor_copy(
+        nc.scalar.copy(
             w2_bf[:].rearrange("p t m j -> p m j t"), w2_raw[:].rearrange("p j (m t) -> p m j t", t=PACK)
         )
         w2_codes = keep.tile([P, H], U32, name="w2_codes", align_bytes=64)
@@ -103,7 +103,7 @@ def tile_picked_ydintg_dif_p_kernel(
         shift = keep.tile([P, PACK, V], F32, name="shift")
         ye_banks = []
         for pair in range(2):
-            ye = psum.tile([P, 2, V], F32, name="ye", tag="turned", bufs=3)
+            ye = psum.tile([P, 2, V], F32, name="ye", tag="turned", bufs=2)
             ye_banks.append(ye)
             for s in range(2):
                 cols = slice((2 * pair + s) * P, (2 * pair + s + 1) * P)
@@ -139,8 +139,9 @@ def tile_picked_ydintg_dif_p_kernel(
         w3_codes = keep.tile([P, N], U32, name="w3_codes", align_bytes=64)
         w3_scales = keep.tile([P, N], U8, name="w3_scales", align_bytes=64)
 
-        picked = keep.tile([P, PACK, U], F32, name="picked")
+        picked = [keep.tile([P, PACK, U // 2], F32, name="picked%d" % g) for g in range(2)]
         ys = {}
+        prods = {}
         atts = {}
 
         def over_d(ap):
@@ -151,7 +152,7 @@ def tile_picked_ydintg_dif_p_kernel(
             cols = slice(t * P, (t + 1) * P)
             js = slice(h * HALF * D, (h + 1) * HALF * D)
             vs = slice(h * HALF, (h + 1) * HALF)
-            y = psum.tile([P, HALF * D], F32, name="y", tag="y", bufs=5)
+            y = psum.tile([P, HALF * D], F32, name="y", tag="y", bufs=6)
             nc.tensor.matmul_mx(
                 y[:], lhsT=w1_codes[:, cols].bitcast(FP8X4), lhsT_scale=w1_scales[:, cols],
                 rhs=x_codes[:, js].bitcast(FP8X4), rhs_scale=x_scale_plane[:, js], start=True, stop=True,
@@ -162,9 +163,15 @@ def tile_picked_ydintg_dif_p_kernel(
             else:
                 prod = ring.tile([P, D, HALF], F32, name="prod")
             nc.vector.tensor_tensor(prod[:], ys[u], over_d(slope[:, t, vs]), ALU.mult)
+            prods[u] = prod
+
+        def attend(u):
+            t, h = divmod(u, 2)
+            vs = slice(h * HALF, (h + 1) * HALF)
+            prod = prods[u]
             if u == units - 1:
-                logit = picked[:, 1, :].rearrange("p (d v) -> p d v", d=D)
-                att = picked[:, 0, :].rearrange("p (d v) -> p d v", d=D)
+                logit = picked[1][:, 0:2, :].rearrange("p t (s v) -> p (t s) v", s=2)
+                att = picked[0][:, 0:2, :].rearrange("p t (s v) -> p (t s) v", s=2)
             else:
                 logit = ring.tile([P, D, HALF], F32, name="logit")
                 att = ring.tile([P, D, HALF], F32, name="att")
@@ -187,7 +194,7 @@ def tile_picked_ydintg_dif_p_kernel(
             ays[u] = ay
 
         def turn(u):
-            bank = psum.tile([P, 2, P], F32, name="bank", tag="turned", bufs=3)
+            bank = psum.tile([P, 2, P], F32, name="bank", tag="turned", bufs=2)
             if u < units:
                 t, h = divmod(u, 2)
                 vs = slice(h * HALF, (h + 1) * HALF)
@@ -208,49 +215,52 @@ def tile_picked_ydintg_dif_p_kernel(
                 nc.scalar.activation(hid_v[:, c0 : c0 + HALF], bank[:, 1, :], ACT.Copy, scale=unit_sb[:, t : t + 1])
 
         units = 2 * PACK
-        weigh_lag = 2
-        turn_lag = 5
+        weigh_lag = 4
+        turn_lag = 6
         for step in range(units + turn_lag + 1):
             if step < units:
                 front(step)
+            if 1 <= step <= units:
+                attend(step - 1)
             if weigh_lag <= step < units + weigh_lag:
                 weigh(step - weigh_lag)
             if step >= turn_lag:
                 turn(step - turn_lag)
-            if step == units - 1:
+            if step == units:
                 w3_bf = keep.tile([P, N, PACK], BF16, name="w3_bf", tag="last_prod", align_bytes=64)
                 nc.scalar.copy(w3_bf[:], w3_raw[:].rearrange("p j n -> p n j"))
                 nc.vector.quantize_mx(w3_codes[:].bitcast(FP8X4), w3_scales[:], w3_bf[:].rearrange("p n j -> p (n j)"))
 
-        hid_bf = keep.tile([P, U, PACK], BF16, name="hid_bf", align_bytes=64)
-        halves = [slice(h * U // 2, (h + 1) * U // 2) for h in range(2)]
-        for t, h in ((0, 0), (1, 0), (2, 0), (0, 1), (3, 0), (1, 1), (2, 1), (3, 1)):
+        hid_bf = [keep.tile([P, U // 2, PACK], BF16, name="hid_bf%d" % g, align_bytes=64) for g in range(2)]
+        parts = (slice(0, U // 2), slice(U // 2, U))
+        order = [(0, 0), (1, 0), (0, 1), (2, 0), (1, 1), (3, 0), (2, 1), (3, 1)]
+        for t, g in order:
             c0 = (PACK - 1 - t) * V
+            rs = parts[g]
             nc.vector.tensor_copy(
-                picked[:, t, halves[h]], hid_v[:, c0 : c0 + WINDOW].indirect(imp_sb[:, h * 16 : (h + 1) * 16])
+                picked[g][:, t, :], hid_v[:, c0 : c0 + WINDOW].indirect(imp_sb[:, rs.start // 16 : rs.stop // 16])
             )
-        planes = picked[:].rearrange("p t r -> p r t")
-        nc.scalar.copy(hid_bf[:, 0:256, :], planes[:, 0:256, :])
-        nc.scalar.copy(hid_bf[:, 256:352, :], planes[:, 256:352, :])
-        nc.vector.tensor_copy(hid_bf[:, 352:512, :], planes[:, 352:512, :])
+        planes = [tile[:].rearrange("p t r -> p r t") for tile in picked]
+        nc.scalar.copy(hid_bf[0][:], planes[0])
+        nc.scalar.copy(hid_bf[1][:, :64, :], planes[1][:, :64, :])
+        nc.vector.tensor_copy(hid_bf[1][:, 64:, :], planes[1][:, 64:, :])
 
         hid_codes = keep.tile([P, U], U32, name="hid_codes", align_bytes=64)
         hid_scales = keep.tile([P, U], U8, name="hid_scales", align_bytes=64)
-        for h in range(2):
-            rs = slice(h * U // 2, (h + 1) * U // 2)
+        for g, rs in enumerate(parts):
             nc.vector.quantize_mx(
-                hid_codes[:, rs].bitcast(FP8X4), hid_scales[:, rs], hid_bf[:, rs, :].rearrange("p r t -> p (r t)")
+                hid_codes[:, rs].bitcast(FP8X4), hid_scales[:, rs], hid_bf[g][:].rearrange("p r t -> p (r t)")
             )
-        for h in range(2):
-            rs = slice(h * U // 2, (h + 1) * U // 2)
-            acc = psum.tile([P, U // 2], F32, name="acc", tag="y", bufs=5)
+        for g, rs in enumerate(parts):
+            width = rs.stop - rs.start
+            acc = psum.tile([P, width], F32, name="acc", tag="y", bufs=6)
             nc.tensor.matmul_mx(
                 acc[:], lhsT=w3_codes[:].bitcast(FP8X4), lhsT_scale=w3_scales[:],
                 rhs=hid_codes[:, rs].bitcast(FP8X4), rhs_scale=hid_scales[:, rs], start=True, stop=True,
             )
-            res = keep.tile([P, U // 2], F32, name="res%d" % h)
-            if h == 0:
-                nc.scalar.copy(res[:], acc[:])
-            else:
+            res = keep.tile([P, width], F32, name="res%d" % g)
+            if g == 1:
                 nc.vector.tensor_copy(res[:], acc[:])
+            else:
+                nc.scalar.copy(res[:], acc[:])
             nc.sync.dma_start(out[:, rs], res[:])

@@ -13,13 +13,28 @@ FP8X4 = mybir.dt.float8_e4m3fn_x4
 ALU = mybir.AluOpType
 ACT = mybir.ActivationFunctionType
 
+K, T, S, D, N, H, V, W, U = 512, 4096, 1024, 4, 128, 512, 256, 1024, 512
+FLOPS = 2 * K * H * S + 2 * K * H * V + 2 * H * N * U
+
 P = 128
 PACK = 4
-K, T, S, D, N, H, V, W, U = 512, 4096, 1024, 4, 128, 512, 256, 1024, 512
-HALF = 128
-WINDOW = 512
-ON_VECTOR = (1, 3)
-FLOPS = 2 * K * H * S + 2 * K * H * V + 2 * H * N * U
+LIST_ROWS = 16
+QUADRANTS = 4
+QUADRANT = P // QUADRANTS
+SCALE_ROWS = 4
+SPREAD = 8
+TARGETS = V // 2
+PARTS = 2 * PACK
+HALF_U = U // 2
+WINDOW = 2 * V
+BANKS = 8
+RING = 6
+
+SHIFT_ON_VECTOR = (1, 3)
+WEIGH_LAG = 4
+TURN_LAG = 6
+GATHER_LAG = 2
+SCALAR_SHARE = 64
 
 
 def tile_picked_ydintg_dif_p_kernel(
@@ -28,12 +43,12 @@ def tile_picked_ydintg_dif_p_kernel(
     nc = tc.nc
     with ExitStack() as ctx:
         keep = ctx.enter_context(tc.tile_pool(name="keep", bufs=1))
-        ring = ctx.enter_context(tc.tile_pool(name="ring", bufs=6))
+        ring = ctx.enter_context(tc.tile_pool(name="ring", bufs=RING))
         psum = ctx.enter_context(tc.psum_pool(name="psum", bufs=1))
 
-        offs_sb = keep.tile([P, S // 16], U16, name="offs_sb")
-        tgt_sb = keep.tile([P, V // 16], U16, name="tgt_sb")
-        imp_sb = keep.tile([P, U // 16], U16, name="imp_sb")
+        offs_sb = keep.tile([P, S // LIST_ROWS], U16, name="offs_sb")
+        tgt_sb = keep.tile([P, V // LIST_ROWS], U16, name="tgt_sb")
+        imp_sb = keep.tile([P, U // LIST_ROWS], U16, name="imp_sb")
         nc.sync.dma_start(tgt_sb[:], tgt)
         nc.sync.dma_start(offs_sb[:], offs)
 
@@ -45,24 +60,21 @@ def tile_picked_ydintg_dif_p_kernel(
         nc.sync.dma_start(e_table[:], e_words[0].rearrange("p n t -> p (n t)").bitcast(I32))
         w2_raw = keep.tile([P, PACK, H], F32, name="w2_raw")
         nc.sync.dma_start(w2_raw[:], w2.rearrange("(p j) c -> p j c", j=PACK))
-        nc.sync.dma_start(x_scale_table[0:P:8, :].bitcast(I32), x_scales[0].bitcast(I32))
-        for q in range(4):
-            queue = nc.gpsimd if q == 3 else nc.sync
+        nc.sync.dma_start(x_scale_table[0:P:SPREAD, :].bitcast(I32), x_scales[0].bitcast(I32))
+        for q in range(QUADRANTS):
+            queue = nc.gpsimd if q == QUADRANTS - 1 else nc.sync
             queue.dma_start(
-                e_scale_table[32 * q : 32 * q + 4, :].bitcast(I32), e_scales[0, 4 * q : 4 * q + 4, :].bitcast(I32)
+                e_scale_table[QUADRANT * q : QUADRANT * q + SCALE_ROWS, :].bitcast(I32),
+                e_scales[0, SCALE_ROWS * q : SCALE_ROWS * (q + 1), :].bitcast(I32),
             )
         nc.sync.dma_start(imp_sb[:], imp)
 
-        warm_in = keep.tile([P, 1], F32, name="warm_in", tag="w1_raw")
-        warm_out = keep.tile([P, 1], F32, name="warm_out", tag="x_table")
-        nc.vector.memset(warm_in[:], 0.0)
-        nc.scalar.activation(warm_out[:], warm_in[:], ACT.Sigmoid)
-        w1_raw = keep.tile([P, PACK, H], F32, name="w1_raw", tag="w1_raw")
+        w1_raw = keep.tile([P, PACK, H], F32, name="w1_raw")
         nc.sync.dma_start(w1_raw[:], w1.rearrange("(p j) c -> p j c", j=PACK))
-        x_table = keep.tile([P, T], I32, name="x_table", tag="x_table")
+        x_table = keep.tile([P, T], I32, name="x_table")
         nc.sync.dma_start(x_table[:], x_words[0].rearrange("p n t -> p (n t)").bitcast(I32))
-        x_scale_plane = keep.tile([P, S], U8, name="x_scale_plane", align_bytes=64)
-        nc.vector.memset(x_scale_plane[:].bitcast(I32), 0)
+        x_code_scales = keep.tile([P, S], U8, name="x_code_scales", align_bytes=64)
+        nc.vector.memset(x_code_scales[:].bitcast(I32), 0)
 
         wp_sb = keep.tile([P, PACK], F32, name="wp_sb")
         wd_sb = keep.tile([P, PACK], F32, name="wd_sb")
@@ -72,44 +84,46 @@ def tile_picked_ydintg_dif_p_kernel(
         nc.gpsimd.dma_start(unit_sb[:], unit.rearrange("(p t) o -> p (t o)", t=PACK))
         ident = keep.tile([P, P], F32, name="ident")
         make_identity(nc, ident[:])
+
         hid_v = keep.tile([P, (PACK - 1) * V + WINDOW], F32, name="hid_v")
         nc.gpsimd.memset(hid_v[:, PACK * V :], 0.0)
 
+        def hid_v_start(t):
+            return (PACK - 1 - t) * V
+
         x_scale_picked = keep.tile([P, S], U8, name="x_scale_picked")
         nc.vector.tensor_copy(x_scale_picked[:], x_scale_table[:].indirect(offs_sb[:]))
-        for q in range(4):
+        for q in range(QUADRANTS):
             nc.sync.dma_start(
-                x_scale_plane[32 * q : 32 * q + 4, :].bitcast(I32),
-                x_scale_picked[32 * q : 32 * q + 32 : 8, :].bitcast(I32),
+                x_code_scales[QUADRANT * q : QUADRANT * q + SCALE_ROWS, :].bitcast(I32),
+                x_scale_picked[QUADRANT * q : QUADRANT * (q + 1) : SPREAD, :].bitcast(I32),
             )
         e_codes = keep.tile([P, V], U32, name="e_codes", align_bytes=64)
         nc.vector.tensor_copy(e_codes[:], e_table[:].bitcast(U32).indirect(tgt_sb[:]))
-        e_scale_plane = keep.tile([P, V], U8, name="e_scale_plane", align_bytes=64)
-        nc.vector.tensor_copy(e_scale_plane[:], e_scale_table[:].indirect(tgt_sb[:]))
+        e_code_scales = keep.tile([P, V], U8, name="e_code_scales", align_bytes=64)
+        nc.vector.tensor_copy(e_code_scales[:], e_scale_table[:].indirect(tgt_sb[:]))
 
-        w2_bf = keep.tile([P, PACK, P, PACK], BF16, name="w2_bf", tag="w_second", align_bytes=64)
-        nc.scalar.copy(
-            w2_bf[:].rearrange("p t m j -> p m j t"), w2_raw[:].rearrange("p j (m t) -> p m j t", t=PACK)
-        )
+        w2_bf = keep.tile([P, PACK, P, PACK], BF16, name="w2_bf", tag="w2_bf_then_w3_raw", align_bytes=64)
+        nc.scalar.copy(w2_bf[:].rearrange("p t m j -> p m j t"), w2_raw[:].rearrange("p j (m t) -> p m j t", t=PACK))
         w2_codes = keep.tile([P, H], U32, name="w2_codes", align_bytes=64)
         w2_scales = keep.tile([P, H], U8, name="w2_scales", align_bytes=64)
         nc.vector.quantize_mx(w2_codes[:].bitcast(FP8X4), w2_scales[:], w2_bf[:].rearrange("p t m j -> p (t m j)"))
 
-        w3_raw = keep.tile([P, PACK, N], F32, name="w3_raw", tag="w_second", align_bytes=64)
+        w3_raw = keep.tile([P, PACK, N], F32, name="w3_raw", tag="w2_bf_then_w3_raw", align_bytes=64)
         nc.sync.dma_start(w3_raw[:], w3.rearrange("(p j) c -> p j c", j=PACK))
 
         neg_ye = keep.tile([P, PACK, V], F32, name="neg_ye")
         slope = keep.tile([P, PACK, V], F32, name="slope")
         shift = keep.tile([P, PACK, V], F32, name="shift")
         ye_banks = []
-        for pair in range(2):
-            ye = psum.tile([P, 2, V], F32, name="ye", tag="turned", bufs=2)
+        for pair in range(PACK // 2):
+            ye = psum.tile([P, 2, V], F32, name="ye", tag="bank", bufs=BANKS)
             ye_banks.append(ye)
             for s in range(2):
                 cols = slice((2 * pair + s) * P, (2 * pair + s + 1) * P)
                 nc.tensor.matmul_mx(
                     ye[:, s, :], lhsT=w2_codes[:, cols].bitcast(FP8X4), lhsT_scale=w2_scales[:, cols],
-                    rhs=e_codes[:].bitcast(FP8X4), rhs_scale=e_scale_plane[:], start=True, stop=True,
+                    rhs=e_codes[:].bitcast(FP8X4), rhs_scale=e_code_scales[:], start=True, stop=True,
                 )
             nc.scalar.activation(neg_ye[:, 2 * pair : 2 * pair + 2, :], ye[:], ACT.Copy, scale=-1.0)
             for s in range(2):
@@ -118,8 +132,8 @@ def tile_picked_ydintg_dif_p_kernel(
                     slope[:, t, :], ye[:, s, :], ACT.Identity, bias=wd_sb[:, t : t + 1], scale=wp_sb[:, t : t + 1]
                 )
                 for h in range(2):
-                    if 2 * t + h not in ON_VECTOR:
-                        vs = slice(h * HALF, (h + 1) * HALF)
+                    if 2 * t + h not in SHIFT_ON_VECTOR:
+                        vs = slice(h * TARGETS, (h + 1) * TARGETS)
                         nc.scalar.activation(shift[:, t, vs], ye[:, s, vs], ACT.Copy, scale=wd_sb[:, t : t + 1])
 
         w1_bf = keep.tile([P, PACK, P, PACK], BF16, name="w1_bf", align_bytes=64)
@@ -131,73 +145,72 @@ def tile_picked_ydintg_dif_p_kernel(
         nc.vector.quantize_mx(w1_codes[:].bitcast(FP8X4), w1_scales[:], w1_bf[:].rearrange("p t m j -> p (t m j)"))
 
         x_codes = keep.tile([P, S], U32, name="x_codes", align_bytes=64)
-        for h in range(2):
-            nc.vector.tensor_copy(
-                x_codes[:, h * 512 : (h + 1) * 512], x_table[:].bitcast(U32).indirect(offs_sb[:, h * 32 : (h + 1) * 32])
-            )
+        behaviours = [slice(h * TARGETS * D, (h + 1) * TARGETS * D) for h in range(2)]
+        for js in behaviours:
+            entries = offs_sb[:, js.start // LIST_ROWS : js.stop // LIST_ROWS]
+            nc.vector.tensor_copy(x_codes[:, js], x_table[:].bitcast(U32).indirect(entries))
 
         w3_codes = keep.tile([P, N], U32, name="w3_codes", align_bytes=64)
         w3_scales = keep.tile([P, N], U8, name="w3_scales", align_bytes=64)
 
-        picked = [keep.tile([P, PACK, U // 2], F32, name="picked%d" % g) for g in range(2)]
+        picked = [keep.tile([P, PACK, HALF_U], F32, name="picked%d" % g) for g in range(2)]
+
         ys = {}
         prods = {}
         atts = {}
+        ays = {}
+        positives = {}
 
         def over_d(ap):
-            return ap.unsqueeze(1).to_broadcast([P, D, HALF])
+            return ap.unsqueeze(1).to_broadcast([P, D, TARGETS])
 
-        def front(u):
+        def multiply(u):
             t, h = divmod(u, 2)
             cols = slice(t * P, (t + 1) * P)
-            js = slice(h * HALF * D, (h + 1) * HALF * D)
-            vs = slice(h * HALF, (h + 1) * HALF)
-            y = psum.tile([P, HALF * D], F32, name="y", tag="y", bufs=6)
+            js = behaviours[h]
+            vs = slice(h * TARGETS, (h + 1) * TARGETS)
+            y = psum.tile([P, TARGETS * D], F32, name="y", tag="bank", bufs=BANKS)
             nc.tensor.matmul_mx(
                 y[:], lhsT=w1_codes[:, cols].bitcast(FP8X4), lhsT_scale=w1_scales[:, cols],
-                rhs=x_codes[:, js].bitcast(FP8X4), rhs_scale=x_scale_plane[:, js], start=True, stop=True,
+                rhs=x_codes[:, js].bitcast(FP8X4), rhs_scale=x_code_scales[:, js], start=True, stop=True,
             )
             ys[u] = y[:].rearrange("p (v d) -> p d v", d=D)
-            if u == units - 1:
-                prod = keep.tile([P, D, HALF], F32, name="last_prod", tag="last_prod", align_bytes=64)
+            if u == PARTS - 1:
+                prod = keep.tile([P, D, TARGETS], F32, name="last_prod", tag="last_prod_then_w3_bf", align_bytes=64)
             else:
-                prod = ring.tile([P, D, HALF], F32, name="prod")
+                prod = ring.tile([P, D, TARGETS], F32, name="prod")
             nc.vector.tensor_tensor(prod[:], ys[u], over_d(slope[:, t, vs]), ALU.mult)
             prods[u] = prod
 
         def attend(u):
             t, h = divmod(u, 2)
-            vs = slice(h * HALF, (h + 1) * HALF)
-            prod = prods[u]
-            if u == units - 1:
+            vs = slice(h * TARGETS, (h + 1) * TARGETS)
+            if u == PARTS - 1:
                 logit = picked[1][:, 0:2, :].rearrange("p t (s v) -> p (t s) v", s=2)
                 att = picked[0][:, 0:2, :].rearrange("p t (s v) -> p (t s) v", s=2)
             else:
-                logit = ring.tile([P, D, HALF], F32, name="logit")
-                att = ring.tile([P, D, HALF], F32, name="att")
-            if u in ON_VECTOR:
+                logit = ring.tile([P, D, TARGETS], F32, name="logit")
+                att = ring.tile([P, D, TARGETS], F32, name="att")
+            if u in SHIFT_ON_VECTOR:
                 nc.vector.scalar_tensor_tensor(
-                    logit[:], over_d(ye_banks[0][:, t, vs]), wd_sb[:, t : t + 1], prod[:], ALU.mult, ALU.subtract
+                    logit[:], over_d(ye_banks[0][:, t, vs]), wd_sb[:, t : t + 1], prods[u][:], ALU.mult, ALU.subtract
                 )
                 nc.scalar.activation(att[:], logit[:], ACT.Sigmoid, scale=-1.0)
             else:
-                nc.gpsimd.tensor_tensor(logit[:], prod[:], over_d(shift[:, t, vs]), ALU.subtract)
+                nc.gpsimd.tensor_tensor(logit[:], prods[u][:], over_d(shift[:, t, vs]), ALU.subtract)
                 nc.scalar.activation(att[:], logit[:], ACT.Sigmoid)
             atts[u] = att
 
-        ays = {}
-        positives = {}
-
         def weigh(u):
-            ay = ring.tile([P, D, HALF], F32, name="ay")
+            ay = ring.tile([P, D, TARGETS], F32, name="ay")
             nc.vector.tensor_tensor(ay[:], ys[u], atts[u][:], ALU.mult)
             ays[u] = ay
 
         def turn(u):
-            bank = psum.tile([P, 2, P], F32, name="bank", tag="turned", bufs=2)
-            if u < units:
+            bank = psum.tile([P, 2, P], F32, name="bank", tag="bank", bufs=BANKS)
+            if u < PARTS:
                 t, h = divmod(u, 2)
-                vs = slice(h * HALF, (h + 1) * HALF)
+                vs = slice(h * TARGETS, (h + 1) * TARGETS)
                 nc.tensor.matmul(bank[:, 0, :], neg_ye[:, t, vs], ident[:], start=True, stop=False, is_transpose=True)
                 for d in range(D):
                     nc.tensor.matmul(
@@ -205,62 +218,67 @@ def tile_picked_ydintg_dif_p_kernel(
                     )
             if u > 0:
                 nc.tensor.transpose(bank[:, 1, :], positives[u - 1][:], ident[:])
-            if u < units:
+            if u < PARTS:
                 pos = ring.tile([P, P], F32, name="pos")
                 nc.scalar.activation(pos[:], bank[:, 0, :], ACT.Relu)
                 positives[u] = pos
             if u > 0:
                 t, h = divmod(u - 1, 2)
-                c0 = (PACK - 1 - t) * V + h * HALF
-                nc.scalar.activation(hid_v[:, c0 : c0 + HALF], bank[:, 1, :], ACT.Copy, scale=unit_sb[:, t : t + 1])
+                c0 = hid_v_start(t) + h * TARGETS
+                nc.scalar.activation(hid_v[:, c0 : c0 + TARGETS], bank[:, 1, :], ACT.Copy, scale=unit_sb[:, t : t + 1])
 
-        units = 2 * PACK
-        weigh_lag = 4
-        turn_lag = 6
-        for step in range(units + turn_lag + 1):
-            if step < units:
-                front(step)
-            if 1 <= step <= units:
+        def quantize_w3():
+            w3_bf = keep.tile([P, N, PACK], BF16, name="w3_bf", tag="last_prod_then_w3_bf", align_bytes=64)
+            nc.scalar.copy(w3_bf[:], w3_raw[:].rearrange("p j n -> p n j"))
+            nc.vector.quantize_mx(w3_codes[:].bitcast(FP8X4), w3_scales[:], w3_bf[:].rearrange("p n j -> p (n j)"))
+
+        for step in range(PARTS + TURN_LAG + 1):
+            if step < PARTS:
+                multiply(step)
+            if 1 <= step <= PARTS:
                 attend(step - 1)
-            if weigh_lag <= step < units + weigh_lag:
-                weigh(step - weigh_lag)
-            if step >= turn_lag:
-                turn(step - turn_lag)
-            if step == units:
-                w3_bf = keep.tile([P, N, PACK], BF16, name="w3_bf", tag="last_prod", align_bytes=64)
-                nc.scalar.copy(w3_bf[:], w3_raw[:].rearrange("p j n -> p n j"))
-                nc.vector.quantize_mx(w3_codes[:].bitcast(FP8X4), w3_scales[:], w3_bf[:].rearrange("p n j -> p (n j)"))
+            if WEIGH_LAG <= step < PARTS + WEIGH_LAG:
+                weigh(step - WEIGH_LAG)
+            if step >= TURN_LAG:
+                turn(step - TURN_LAG)
+            if step == PARTS:
+                quantize_w3()
 
-        hid_bf = [keep.tile([P, U // 2, PACK], BF16, name="hid_bf%d" % g, align_bytes=64) for g in range(2)]
-        parts = (slice(0, U // 2), slice(U // 2, U))
-        order = [(0, 0), (1, 0), (0, 1), (2, 0), (1, 1), (3, 0), (2, 1), (3, 1)]
-        for t, g in order:
-            c0 = (PACK - 1 - t) * V
-            rs = parts[g]
-            nc.vector.tensor_copy(
-                picked[g][:, t, :], hid_v[:, c0 : c0 + WINDOW].indirect(imp_sb[:, rs.start // 16 : rs.stop // 16])
-            )
-        planes = [tile[:].rearrange("p t r -> p r t") for tile in picked]
-        nc.scalar.copy(hid_bf[0][:], planes[0])
-        nc.scalar.copy(hid_bf[1][:, :64, :], planes[1][:, :64, :])
-        nc.vector.tensor_copy(hid_bf[1][:, 64:, :], planes[1][:, 64:, :])
+        hid_bf = [keep.tile([P, HALF_U, PACK], BF16, name="hid_bf%d" % g, align_bytes=64) for g in range(2)]
+        impressions = [slice(g * HALF_U, (g + 1) * HALF_U) for g in range(2)]
+
+        def gather(t, g):
+            window = hid_v[:, hid_v_start(t) : hid_v_start(t) + WINDOW]
+            entries = imp_sb[:, impressions[g].start // LIST_ROWS : impressions[g].stop // LIST_ROWS]
+            nc.vector.tensor_copy(picked[g][:, t, :], window.indirect(entries))
+
+        for step in range(PACK + GATHER_LAG):
+            if step >= GATHER_LAG:
+                gather(step - GATHER_LAG, 1)
+            if step < PACK:
+                gather(step, 0)
+
+        by_impression = [tile[:].rearrange("p t r -> p r t") for tile in picked]
+        nc.scalar.copy(hid_bf[0][:], by_impression[0])
+        nc.scalar.copy(hid_bf[1][:, :SCALAR_SHARE, :], by_impression[1][:, :SCALAR_SHARE, :])
+        nc.vector.tensor_copy(hid_bf[1][:, SCALAR_SHARE:, :], by_impression[1][:, SCALAR_SHARE:, :])
 
         hid_codes = keep.tile([P, U], U32, name="hid_codes", align_bytes=64)
         hid_scales = keep.tile([P, U], U8, name="hid_scales", align_bytes=64)
-        for g, rs in enumerate(parts):
+        for g, rs in enumerate(impressions):
             nc.vector.quantize_mx(
                 hid_codes[:, rs].bitcast(FP8X4), hid_scales[:, rs], hid_bf[g][:].rearrange("p r t -> p (r t)")
             )
-        for g, rs in enumerate(parts):
-            width = rs.stop - rs.start
-            acc = psum.tile([P, width], F32, name="acc", tag="y", bufs=6)
+
+        for g, rs in enumerate(impressions):
+            acc = psum.tile([P, HALF_U], F32, name="acc", tag="bank", bufs=BANKS)
             nc.tensor.matmul_mx(
                 acc[:], lhsT=w3_codes[:].bitcast(FP8X4), lhsT_scale=w3_scales[:],
                 rhs=hid_codes[:, rs].bitcast(FP8X4), rhs_scale=hid_scales[:, rs], start=True, stop=True,
             )
-            res = keep.tile([P, width], F32, name="res%d" % g)
-            if g == 1:
-                nc.vector.tensor_copy(res[:], acc[:])
-            else:
+            res = keep.tile([P, HALF_U], F32, name="res%d" % g)
+            if g == 0:
                 nc.scalar.copy(res[:], acc[:])
+            else:
+                nc.vector.tensor_copy(res[:], acc[:])
             nc.sync.dma_start(out[:, rs], res[:])

from contextlib import ExitStack

import concourse.mybir as mybir
from concourse.masks import make_identity

F32 = mybir.dt.float32
BF16 = mybir.dt.bfloat16
I32 = mybir.dt.int32
U32 = mybir.dt.uint32
U16 = mybir.dt.uint16
U8 = mybir.dt.uint8
FP8X4 = mybir.dt.float8_e4m3fn_x4
ALU = mybir.AluOpType
ACT = mybir.ActivationFunctionType

K, T, S, D, N, H, V, W, U = 512, 4096, 1024, 4, 128, 512, 256, 1024, 512
FLOPS = 2 * K * H * S + 2 * K * H * V + 2 * H * N * U

P = 128
PACK = 4
LIST_ROWS = 16
QUADRANTS = 4
QUADRANT = P // QUADRANTS
SCALE_ROWS = 4
SPREAD = 8
TARGETS = V // 2
PARTS = 2 * PACK
HALF_U = U // 2
WINDOW = 2 * V
BANKS = 8
RING = 6

SHIFT_ON_VECTOR = (1, 3)
WEIGH_LAG = 4
TURN_LAG = 6
GATHER_LAG = 2
SCALAR_SHARE = 64


def tile_picked_ydintg_dif_p_kernel(
    tc, x_words, x_scales, w1, e_words, e_scales, w2, wp, wd, unit, w3, offs, tgt, imp, out
):
    nc = tc.nc
    with ExitStack() as ctx:
        keep = ctx.enter_context(tc.tile_pool(name="keep", bufs=1))
        ring = ctx.enter_context(tc.tile_pool(name="ring", bufs=RING))
        psum = ctx.enter_context(tc.psum_pool(name="psum", bufs=1))

        offs_sb = keep.tile([P, S // LIST_ROWS], U16, name="offs_sb")
        tgt_sb = keep.tile([P, V // LIST_ROWS], U16, name="tgt_sb")
        imp_sb = keep.tile([P, U // LIST_ROWS], U16, name="imp_sb")
        nc.sync.dma_start(tgt_sb[:], tgt)
        nc.sync.dma_start(offs_sb[:], offs)

        x_scale_table = keep.tile([P, T], U8, name="x_scale_table")
        nc.vector.memset(x_scale_table[:].bitcast(I32), 0)
        e_scale_table = keep.tile([P, W], U8, name="e_scale_table")
        nc.gpsimd.memset(e_scale_table[:].bitcast(I32), 0)
        e_table = keep.tile([P, W], I32, name="e_table")
        nc.sync.dma_start(e_table[:], e_words[0].rearrange("p n t -> p (n t)").bitcast(I32))
        w2_raw = keep.tile([P, PACK, H], F32, name="w2_raw")
        nc.sync.dma_start(w2_raw[:], w2.rearrange("(p j) c -> p j c", j=PACK))
        nc.sync.dma_start(x_scale_table[0:P:SPREAD, :].bitcast(I32), x_scales[0].bitcast(I32))
        for q in range(QUADRANTS):
            queue = nc.gpsimd if q == QUADRANTS - 1 else nc.sync
            queue.dma_start(
                e_scale_table[QUADRANT * q : QUADRANT * q + SCALE_ROWS, :].bitcast(I32),
                e_scales[0, SCALE_ROWS * q : SCALE_ROWS * (q + 1), :].bitcast(I32),
            )
        nc.sync.dma_start(imp_sb[:], imp)

        w1_raw = keep.tile([P, PACK, H], F32, name="w1_raw")
        nc.sync.dma_start(w1_raw[:], w1.rearrange("(p j) c -> p j c", j=PACK))
        x_table = keep.tile([P, T], I32, name="x_table")
        nc.sync.dma_start(x_table[:], x_words[0].rearrange("p n t -> p (n t)").bitcast(I32))
        x_code_scales = keep.tile([P, S], U8, name="x_code_scales", align_bytes=64)
        nc.vector.memset(x_code_scales[:].bitcast(I32), 0)

        wp_sb = keep.tile([P, PACK], F32, name="wp_sb")
        wd_sb = keep.tile([P, PACK], F32, name="wd_sb")
        unit_sb = keep.tile([P, PACK], F32, name="unit_sb")
        nc.gpsimd.dma_start(wp_sb[:], wp.rearrange("(p t) o -> p (t o)", t=PACK))
        nc.gpsimd.dma_start(wd_sb[:], wd.rearrange("(p t) o -> p (t o)", t=PACK))
        nc.gpsimd.dma_start(unit_sb[:], unit.rearrange("(p t) o -> p (t o)", t=PACK))
        ident = keep.tile([P, P], F32, name="ident")
        make_identity(nc, ident[:])

        hid_v = keep.tile([P, (PACK - 1) * V + WINDOW], F32, name="hid_v")
        nc.gpsimd.memset(hid_v[:, PACK * V :], 0.0)

        def hid_v_start(t):
            return (PACK - 1 - t) * V

        x_scale_picked = keep.tile([P, S], U8, name="x_scale_picked")
        nc.vector.tensor_copy(x_scale_picked[:], x_scale_table[:].indirect(offs_sb[:]))
        for q in range(QUADRANTS):
            nc.sync.dma_start(
                x_code_scales[QUADRANT * q : QUADRANT * q + SCALE_ROWS, :].bitcast(I32),
                x_scale_picked[QUADRANT * q : QUADRANT * (q + 1) : SPREAD, :].bitcast(I32),
            )
        e_codes = keep.tile([P, V], U32, name="e_codes", align_bytes=64)
        nc.vector.tensor_copy(e_codes[:], e_table[:].bitcast(U32).indirect(tgt_sb[:]))
        e_code_scales = keep.tile([P, V], U8, name="e_code_scales", align_bytes=64)
        nc.vector.tensor_copy(e_code_scales[:], e_scale_table[:].indirect(tgt_sb[:]))

        w2_bf = keep.tile([P, PACK, P, PACK], BF16, name="w2_bf", tag="w2_bf_then_w3_raw", align_bytes=64)
        nc.scalar.copy(w2_bf[:].rearrange("p t m j -> p m j t"), w2_raw[:].rearrange("p j (m t) -> p m j t", t=PACK))
        w2_codes = keep.tile([P, H], U32, name="w2_codes", align_bytes=64)
        w2_scales = keep.tile([P, H], U8, name="w2_scales", align_bytes=64)
        nc.vector.quantize_mx(w2_codes[:].bitcast(FP8X4), w2_scales[:], w2_bf[:].rearrange("p t m j -> p (t m j)"))

        w3_raw = keep.tile([P, PACK, N], F32, name="w3_raw", tag="w2_bf_then_w3_raw", align_bytes=64)
        nc.sync.dma_start(w3_raw[:], w3.rearrange("(p j) c -> p j c", j=PACK))

        neg_ye = keep.tile([P, PACK, V], F32, name="neg_ye")
        slope = keep.tile([P, PACK, V], F32, name="slope")
        shift = keep.tile([P, PACK, V], F32, name="shift")
        ye_banks = []
        for pair in range(PACK // 2):
            ye = psum.tile([P, 2, V], F32, name="ye", tag="bank", bufs=BANKS)
            ye_banks.append(ye)
            for s in range(2):
                cols = slice((2 * pair + s) * P, (2 * pair + s + 1) * P)
                nc.tensor.matmul_mx(
                    ye[:, s, :], lhsT=w2_codes[:, cols].bitcast(FP8X4), lhsT_scale=w2_scales[:, cols],
                    rhs=e_codes[:].bitcast(FP8X4), rhs_scale=e_code_scales[:], start=True, stop=True,
                )
            nc.scalar.activation(neg_ye[:, 2 * pair : 2 * pair + 2, :], ye[:], ACT.Copy, scale=-1.0)
            for s in range(2):
                t = 2 * pair + s
                nc.scalar.activation(
                    slope[:, t, :], ye[:, s, :], ACT.Identity, bias=wd_sb[:, t : t + 1], scale=wp_sb[:, t : t + 1]
                )
                for h in range(2):
                    if 2 * t + h not in SHIFT_ON_VECTOR:
                        vs = slice(h * TARGETS, (h + 1) * TARGETS)
                        nc.scalar.activation(shift[:, t, vs], ye[:, s, vs], ACT.Copy, scale=wd_sb[:, t : t + 1])

        w1_bf = keep.tile([P, PACK, P, PACK], BF16, name="w1_bf", align_bytes=64)
        nc.vector.tensor_copy(
            w1_bf[:].rearrange("p t m j -> p m j t"), w1_raw[:].rearrange("p j (m t) -> p m j t", t=PACK)
        )
        w1_codes = keep.tile([P, H], U32, name="w1_codes", align_bytes=64)
        w1_scales = keep.tile([P, H], U8, name="w1_scales", align_bytes=64)
        nc.vector.quantize_mx(w1_codes[:].bitcast(FP8X4), w1_scales[:], w1_bf[:].rearrange("p t m j -> p (t m j)"))

        x_codes = keep.tile([P, S], U32, name="x_codes", align_bytes=64)
        behaviours = [slice(h * TARGETS * D, (h + 1) * TARGETS * D) for h in range(2)]
        for js in behaviours:
            entries = offs_sb[:, js.start // LIST_ROWS : js.stop // LIST_ROWS]
            nc.vector.tensor_copy(x_codes[:, js], x_table[:].bitcast(U32).indirect(entries))

        w3_codes = keep.tile([P, N], U32, name="w3_codes", align_bytes=64)
        w3_scales = keep.tile([P, N], U8, name="w3_scales", align_bytes=64)

        picked = [keep.tile([P, PACK, HALF_U], F32, name="picked%d" % g) for g in range(2)]

        ys = {}
        prods = {}
        atts = {}
        ays = {}
        positives = {}

        def over_d(ap):
            return ap.unsqueeze(1).to_broadcast([P, D, TARGETS])

        def multiply(u):
            t, h = divmod(u, 2)
            cols = slice(t * P, (t + 1) * P)
            js = behaviours[h]
            vs = slice(h * TARGETS, (h + 1) * TARGETS)
            y = psum.tile([P, TARGETS * D], F32, name="y", tag="bank", bufs=BANKS)
            nc.tensor.matmul_mx(
                y[:], lhsT=w1_codes[:, cols].bitcast(FP8X4), lhsT_scale=w1_scales[:, cols],
                rhs=x_codes[:, js].bitcast(FP8X4), rhs_scale=x_code_scales[:, js], start=True, stop=True,
            )
            ys[u] = y[:].rearrange("p (v d) -> p d v", d=D)
            if u == PARTS - 1:
                prod = keep.tile([P, D, TARGETS], F32, name="last_prod", tag="last_prod_then_w3_bf", align_bytes=64)
            else:
                prod = ring.tile([P, D, TARGETS], F32, name="prod")
            nc.vector.tensor_tensor(prod[:], ys[u], over_d(slope[:, t, vs]), ALU.mult)
            prods[u] = prod

        def attend(u):
            t, h = divmod(u, 2)
            vs = slice(h * TARGETS, (h + 1) * TARGETS)
            if u == PARTS - 1:
                logit = picked[1][:, 0:2, :].rearrange("p t (s v) -> p (t s) v", s=2)
                att = picked[0][:, 0:2, :].rearrange("p t (s v) -> p (t s) v", s=2)
            else:
                logit = ring.tile([P, D, TARGETS], F32, name="logit")
                att = ring.tile([P, D, TARGETS], F32, name="att")
            if u in SHIFT_ON_VECTOR:
                nc.vector.scalar_tensor_tensor(
                    logit[:], over_d(ye_banks[0][:, t, vs]), wd_sb[:, t : t + 1], prods[u][:], ALU.mult, ALU.subtract
                )
                nc.scalar.activation(att[:], logit[:], ACT.Sigmoid, scale=-1.0)
            else:
                nc.gpsimd.tensor_tensor(logit[:], prods[u][:], over_d(shift[:, t, vs]), ALU.subtract)
                nc.scalar.activation(att[:], logit[:], ACT.Sigmoid)
            atts[u] = att

        def weigh(u):
            ay = ring.tile([P, D, TARGETS], F32, name="ay")
            nc.vector.tensor_tensor(ay[:], ys[u], atts[u][:], ALU.mult)
            ays[u] = ay

        def turn(u):
            bank = psum.tile([P, 2, P], F32, name="bank", tag="bank", bufs=BANKS)
            if u < PARTS:
                t, h = divmod(u, 2)
                vs = slice(h * TARGETS, (h + 1) * TARGETS)
                nc.tensor.matmul(bank[:, 0, :], neg_ye[:, t, vs], ident[:], start=True, stop=False, is_transpose=True)
                for d in range(D):
                    nc.tensor.matmul(
                        bank[:, 0, :], ays[u][:, d, :], ident[:], start=False, stop=(d == D - 1), is_transpose=True
                    )
            if u > 0:
                nc.tensor.transpose(bank[:, 1, :], positives[u - 1][:], ident[:])
            if u < PARTS:
                pos = ring.tile([P, P], F32, name="pos")
                nc.scalar.activation(pos[:], bank[:, 0, :], ACT.Relu)
                positives[u] = pos
            if u > 0:
                t, h = divmod(u - 1, 2)
                c0 = hid_v_start(t) + h * TARGETS
                nc.scalar.activation(hid_v[:, c0 : c0 + TARGETS], bank[:, 1, :], ACT.Copy, scale=unit_sb[:, t : t + 1])

        def quantize_w3():
            w3_bf = keep.tile([P, N, PACK], BF16, name="w3_bf", tag="last_prod_then_w3_bf", align_bytes=64)
            nc.scalar.copy(w3_bf[:], w3_raw[:].rearrange("p j n -> p n j"))
            nc.vector.quantize_mx(w3_codes[:].bitcast(FP8X4), w3_scales[:], w3_bf[:].rearrange("p n j -> p (n j)"))

        for step in range(PARTS + TURN_LAG + 1):
            if step < PARTS:
                multiply(step)
            if 1 <= step <= PARTS:
                attend(step - 1)
            if WEIGH_LAG <= step < PARTS + WEIGH_LAG:
                weigh(step - WEIGH_LAG)
            if step >= TURN_LAG:
                turn(step - TURN_LAG)
            if step == PARTS:
                quantize_w3()

        hid_bf = [keep.tile([P, HALF_U, PACK], BF16, name="hid_bf%d" % g, align_bytes=64) for g in range(2)]
        impressions = [slice(g * HALF_U, (g + 1) * HALF_U) for g in range(2)]

        def gather(t, g):
            window = hid_v[:, hid_v_start(t) : hid_v_start(t) + WINDOW]
            entries = imp_sb[:, impressions[g].start // LIST_ROWS : impressions[g].stop // LIST_ROWS]
            nc.vector.tensor_copy(picked[g][:, t, :], window.indirect(entries))

        for step in range(PACK + GATHER_LAG):
            if step >= GATHER_LAG:
                gather(step - GATHER_LAG, 1)
            if step < PACK:
                gather(step, 0)

        by_impression = [tile[:].rearrange("p t r -> p r t") for tile in picked]
        nc.scalar.copy(hid_bf[0][:], by_impression[0])
        nc.scalar.copy(hid_bf[1][:, :SCALAR_SHARE, :], by_impression[1][:, :SCALAR_SHARE, :])
        nc.vector.tensor_copy(hid_bf[1][:, SCALAR_SHARE:, :], by_impression[1][:, SCALAR_SHARE:, :])

        hid_codes = keep.tile([P, U], U32, name="hid_codes", align_bytes=64)
        hid_scales = keep.tile([P, U], U8, name="hid_scales", align_bytes=64)
        for g, rs in enumerate(impressions):
            nc.vector.quantize_mx(
                hid_codes[:, rs].bitcast(FP8X4), hid_scales[:, rs], hid_bf[g][:].rearrange("p r t -> p (r t)")
            )

        for g, rs in enumerate(impressions):
            acc = psum.tile([P, HALF_U], F32, name="acc", tag="bank", bufs=BANKS)
            nc.tensor.matmul_mx(
                acc[:], lhsT=w3_codes[:].bitcast(FP8X4), lhsT_scale=w3_scales[:],
                rhs=hid_codes[:, rs].bitcast(FP8X4), rhs_scale=hid_scales[:, rs], start=True, stop=True,
            )
            res = keep.tile([P, HALF_U], F32, name="res%d" % g)
            if g == 0:
                nc.scalar.copy(res[:], acc[:])
            else:
                nc.vector.tensor_copy(res[:], acc[:])
            nc.sync.dma_start(out[:, rs], res[:])
